import numpy as np, ml_dtypes
CORES = [4,12,20,28,44,60,76,84,92,108,116,124]
N = 12
TK = 64
def setup_inputs(rng):
    return {"x": rng.standard_normal((N, 128, TK), dtype=np.float32).astype(ml_dtypes.bfloat16), "w": rng.standard_normal((N, 128, 128), dtype=np.float32).astype(ml_dtypes.bfloat16)}
def setup_inputs_big(rng):
    d = setup_inputs(rng)
    for k in ("x", "w"): d[k] = (d[k].astype(np.float32) * 1024.0).astype(d[k].dtype)
    return d
def setup_inputs_small(rng):
    d = setup_inputs(rng)
    for k in ("x", "w"): d[k] = (d[k].astype(np.float32) * (1 / 1024.0)).astype(d[k].dtype)
    return d
def setup_inputs_apart(rng):
    d = setup_inputs(rng)
    f = (10.0 ** rng.permutation(np.linspace(-1.5, 1.5, N))).astype(np.float32).reshape(N, 1, 1)
    for k in ("x", "w"): d[k] = (d[k].astype(np.float32) * f).astype(d[k].dtype)
    return d
def setup_inputs_neg(rng):
    d = setup_inputs(rng)
    d["x"] = (np.abs(d["x"].astype(np.float32)) * 1048576.0).astype(d["x"].dtype); d["w"] = (-np.abs(d["w"].astype(np.float32))).astype(d["w"].dtype)
    return d
def reference(x, w):
    X, W = x.astype(np.float64), w.astype(np.float64)
    y = np.stack([np.max([W[j].T @ X[r] for j in range(N)], axis=0) for r in range(N)])
    return {"y": y.astype(ml_dtypes.bfloat16)}

@@ -1,0 +1,177 @@
+from concourse.bass import DstId, RemoteDMATransfer
+from concourse.mybir import AluOpType
+
+N = 12
+M = 128
+TK = 64
+NB = 8
+ND = 3
+CAP = 2
+E_CHIP = 8
+
+SCRATCH = {
+    "wd": ("dram", [128, M], "bfloat16"),
+    "wall": ("sbuf", [128, N * M], "bfloat16"),
+    "xs": ("sbuf", [128, TK], "bfloat16"),
+    "acc0": ("sbuf", [128, TK], "float32"),
+    "acc1": ("sbuf", [128, TK], "float32"),
+    "yb": ("sbuf", [128, TK], "bfloat16"),
+}
+for _b in range(NB):
+    SCRATCH["ps%d" % _b] = ("psum", [128, 512], "float32")
+
+SEMAPHORES = (["xl", "wl", "dl", "sent", "st"] + ["a%d" % _j for _j in range(N)]
+              + ["m%d" % _j for _j in range(N)] + ["v%d" % _j for _j in range(N)])
+
+_CACHE = {}
+
+
+def _route(topo, a, b):
+    ca, cb, d = topo.chip(a), topo.chip(b), topo.die(a)
+    if ca == cb:
+        return []
+    if topo.mates(ca, cb):
+        return [("mate", ca, d)]
+    if topo.same_plane(ca, cb):
+        return [("out", ca, d), ("in", cb, d)]
+    m = [k for k in range(topo.CHIPS) if topo.mates(ca, k)][0]
+    return [("mate", ca, d), ("out", m, d), ("in", cb, d)]
+
+
+def _plan(ranks, topo):
+    load = {}
+
+    def add(a, b):
+        for l in _route(topo, a, b):
+            load[l] = load.get(l, 0) + 1
+
+    direct, helpers, todo = {}, {}, []
+    for i, s in enumerate(ranks):
+        rot = ranks[i + 1:] + ranks[:i]
+        own = [d for d in rot if topo.may_write(s, d)]
+        far = [d for d in rot if not topo.may_write(s, d)]
+        direct[s] = own[:ND]
+        for d in direct[s]:
+            add(s, d)
+        todo.append((s, far, own[ND:]))
+    every = range(topo.CHIPS * topo.CORES_PER_CHIP)
+    for s, far, rest in todo:
+        mine = [c for c in every if topo.chip(c) == topo.chip(s) and c != s]
+        opened, order = {}, []
+        for grp in (far, rest):
+            room, fresh = -(-len(grp) // CAP), 0
+            for d in grp:
+                best = None
+                for h in mine:
+                    if not topo.may_write(h, d):
+                        continue
+                    if h in opened:
+                        if len(opened[h]) >= CAP:
+                            continue
+                    elif fresh >= room:
+                        continue
+                    ls = _route(topo, h, d)
+                    key = (max([load.get(l, 0) + 1 for l in ls if l[0] == "in"] + [0]),
+                           max(load.get(l, 0) + 1 for l in ls),
+                           0 if h in opened else 1, topo.die(h) != topo.die(s), h)
+                    if best is None or key < best[0]:
+                        best = (key, h)
+                h = best[1]
+                if h not in opened:
+                    opened[h] = []
+                    order.append(h)
+                    fresh += 1
+                opened[h].append(d)
+                add(h, d)
+        helpers[s] = [(h, opened[h]) for h in order]
+    return direct, helpers
+
+
+def _bits(mask):
+    return bin(mask).count("1")
+
+
+def _mask(topo, me, dests, n=None):
+    mask = topo.mask(me, dests[0])
+    for d in dests:
+        mask &= topo.mask(me, d)
+    if n is not None and n < _bits(mask):
+        on = [b for b in range(mask.bit_length()) if (mask >> b) & 1]
+        mask = sum(1 << b for b in on[::len(on) // n][:n])
+    return mask
+
+
+def _send(g, T, topo, dests, j, mask, out):
+    ids = [DstId(rid=topo.addr(d)[0], pnc=topo.addr(d)[1]) for d in dests]
+    g.remote_dma_fused(
+        [RemoteDMATransfer(dst_ids=ids, dma_engine_mask=mask, remote_sem=T.sem["a%d" % j],
+                           srcs=[T.wd[:]], dsts=[out for _ in dests], alu_op=0)],
+        local_sem=T.sem.sent)
+    return _bits(mask)
+
+
+def rank_program(g, core, T, topo):
+    ranks = list(T.cores)
+    if "plan" not in _CACHE:
+        _CACHE["plan"] = _plan(ranks, topo)
+    direct, helpers = _CACHE["plan"]
+    rank = T.rank_of(core)
+
+    def chip_mask(s):
+        return _mask(topo, s, [h for h, _ in helpers[s]], E_CHIP)
+
+    if rank is None:
+        for j, s in enumerate(ranks):
+            for h, dests in helpers[s]:
+                if h == core:
+                    g.wait_ge(T.sem["a%d" % j], _bits(chip_mask(s)))
+                    n = _send(g, T, topo, dests, j, _mask(topo, core, dests), T.wall[:, j * M:(j + 1) * M])
+                    g.wait_ge(T.sem.sent, n)
+        return
+
+    slot = T.wall[:, rank * M:(rank + 1) * M]
+    g.scalar.dma_start(T.wd[:], T.w[:]).then_inc(T.sem.dl, 16)
+    g.sync.dma_start(T.xs[:], T.x[:]).then_inc(T.sem.xl, 16)
+    g.sync.dma_start(slot, T.w[:]).then_inc(T.sem.wl, 16)
+
+    g.wait_ge(T.sem.dl, 16)
+    n = _send(g, T, topo, [h for h, _ in helpers[core]], rank, chip_mask(core), T.wd[:])
+    n += _send(g, T, topo, direct[core], rank, _mask(topo, core, direct[core]), slot)
+
+    exp = [((0, 0), rank, 0)]
+    for j, s in enumerate(ranks):
+        if core in direct[s]:
+            exp.append(((1, direct[s].index(core)), j, _bits(_mask(topo, s, direct[s]))))
+        for hi, (h, dests) in enumerate(helpers[s]):
+            if core in dests:
+                exp.append(((2, dests.index(core), hi), j, _bits(_mask(topo, h, dests))))
+    exp.sort()
+
+    te, ve = g.tensor, g.vector
+    te.wait_ge(T.sem.xl, 16)
+    for i, (_, j, cnt) in enumerate(exp):
+        if j == rank:
+            te.wait_ge(T.sem.wl, 16)
+        else:
+            te.wait_ge(T.sem["a%d" % j], cnt)
+        if i >= NB:
+            te.wait_ge(T.sem["v%d" % (i - NB)], 1)
+        te.matmul(out=T["ps%d" % (i % NB)][:, 0:TK], lhsT=T.wall[:, j * M:(j + 1) * M], rhs=T.xs[:],
+                  start=True, stop=True).then_inc(T.sem["m%d" % i], 1)
+
+    acc = [T.acc0, T.acc1]
+    for i in range(N):
+        ps = T["ps%d" % (i % NB)][:, 0:TK]
+        ve.wait_ge(T.sem["m%d" % i], 1)
+        if i == 0:
+            ve.tensor_copy(out=acc[0][:], in_=ps).then_inc(T.sem.v0, 1)
+        else:
+            ve.wait_ge(T.sem["v%d" % (i - 1)], 1)
+            out = T.yb if i == N - 1 else acc[i % 2]
+            ve.tensor_tensor(out=out[:], in0=acc[(i - 1) % 2][:], in1=ps,
+                             op=AluOpType.max).then_inc(T.sem["v%d" % i], 1)
+
+    g.sync.wait_ge(T.sem["v%d" % (N - 1)], 1)
+    g.sync.dma_start(T.y[:], T.yb[:]).then_inc(T.sem.st, 16)
+    g.sync.wait_ge(T.sem.st, 16)
+    g.wait_ge(T.sem.sent, n)

@@ -5,9 +5,10 @@ N = 12
 M = 128
 TK = 64
 NB = 8
-ND = 3
+ND = 5
 CAP = 2
-E_CHIP = 8
+E_CHIP = 4
+E_COPY = 4
 
 SCRATCH = {
     "wd": ("dram", [128, M], "bfloat16"),
@@ -39,51 +40,34 @@ def _route(topo, a, b):
 
 
 def _plan(ranks, topo):
-    load = {}
-
-    def add(a, b):
-        for l in _route(topo, a, b):
-            load[l] = load.get(l, 0) + 1
-
-    direct, helpers, todo = {}, {}, []
+    load, direct, helpers = {}, {}, {}
+    every = range(topo.CHIPS * topo.CORES_PER_CHIP)
     for i, s in enumerate(ranks):
         rot = ranks[i + 1:] + ranks[:i]
-        own = [d for d in rot if topo.may_write(s, d)]
+        near = [d for d in rot if topo.may_write(s, d)]
+        direct[s] = near[:ND]
         far = [d for d in rot if not topo.may_write(s, d)]
-        direct[s] = own[:ND]
-        for d in direct[s]:
-            add(s, d)
-        todo.append((s, far, own[ND:]))
-    every = range(topo.CHIPS * topo.CORES_PER_CHIP)
-    for s, far, rest in todo:
-        mine = [c for c in every if topo.chip(c) == topo.chip(s) and c != s]
-        opened, order = {}, []
-        for grp in (far, rest):
-            room, fresh = -(-len(grp) // CAP), 0
-            for d in grp:
-                best = None
-                for h in mine:
-                    if not topo.may_write(h, d):
-                        continue
-                    if h in opened:
-                        if len(opened[h]) >= CAP:
-                            continue
-                    elif fresh >= room:
-                        continue
-                    ls = _route(topo, h, d)
-                    key = (max([load.get(l, 0) + 1 for l in ls if l[0] == "in"] + [0]),
-                           max(load.get(l, 0) + 1 for l in ls),
-                           0 if h in opened else 1, topo.die(h) != topo.die(s), h)
-                    if best is None or key < best[0]:
-                        best = (key, h)
-                h = best[1]
-                if h not in opened:
-                    opened[h] = []
-                    order.append(h)
-                    fresh += 1
-                opened[h].append(d)
-                add(h, d)
-        helpers[s] = [(h, opened[h]) for h in order]
+        own = [c for c in every if topo.chip(c) == topo.chip(s) and c != s
+               and all(topo.may_write(c, d) for d in far)]
+        cap = -(-len(far) // len(own))
+        opened = {}
+        for d in far + near[ND:]:
+            best = None
+            for h in own:
+                if d in far and len(opened.get(h, [])) >= cap:
+                    continue
+                if d not in far and (len(opened.get(h, [])) >= CAP or topo.die(h) == topo.die(s)):
+                    continue
+                ls = _route(topo, h, d)
+                key = (max([load.get(l, 0) + 1 for l in ls if l[0] == "in"] + [0]),
+                       max(load.get(l, 0) + 1 for l in ls), len(opened.get(h, [])), h)
+                if best is None or key < best[0]:
+                    best = (key, h)
+            h = best[1]
+            opened.setdefault(h, []).append(d)
+            for l in _route(topo, h, d):
+                load[l] = load.get(l, 0) + 1
+        helpers[s] = sorted(opened.items())
     return direct, helpers
 
 
@@ -91,13 +75,17 @@ def _bits(mask):
     return bin(mask).count("1")
 
 
-def _mask(topo, me, dests, n=None):
+def _thin(mask, n):
+    if n < _bits(mask):
+        on = [b for b in range(mask.bit_length()) if (mask >> b) & 1]
+        mask = sum(1 << b for b in on[::len(on) // n][:n])
+    return mask
+
+
+def _mask(topo, me, dests):
     mask = topo.mask(me, dests[0])
     for d in dests:
         mask &= topo.mask(me, d)
-    if n is not None and n < _bits(mask):
-        on = [b for b in range(mask.bit_length()) if (mask >> b) & 1]
-        mask = sum(1 << b for b in on[::len(on) // n][:n])
     return mask
 
 
@@ -118,19 +106,23 @@ def rank_program(g, core, T, topo):
     rank = T.rank_of(core)
 
     def chip_mask(s):
-        return _mask(topo, s, [h for h, _ in helpers[s]], E_CHIP)
+        return _thin(_mask(topo, s, [h for h, _ in helpers[s]]) & ~_mask(topo, s, direct[s]), E_CHIP)
+
+    def pass_mask(h, dests):
+        return _thin(_mask(topo, h, dests), E_COPY * len(dests))
 
     if rank is None:
         for j, s in enumerate(ranks):
             for h, dests in helpers[s]:
                 if h == core:
                     g.wait_ge(T.sem["a%d" % j], _bits(chip_mask(s)))
-                    n = _send(g, T, topo, dests, j, _mask(topo, core, dests), T.wall[:, j * M:(j + 1) * M])
+                    n = _send(g, T, topo, dests, j, pass_mask(core, dests), T.wall[:, j * M:(j + 1) * M])
                     g.wait_ge(T.sem.sent, n)
         return
 
     slot = T.wall[:, rank * M:(rank + 1) * M]
     g.scalar.dma_start(T.wd[:], T.w[:]).then_inc(T.sem.dl, 16)
+    g.sync.wait_ge(T.sem.dl, 16)
     g.sync.dma_start(T.xs[:], T.x[:]).then_inc(T.sem.xl, 16)
     g.sync.dma_start(slot, T.w[:]).then_inc(T.sem.wl, 16)
 
@@ -141,10 +133,10 @@ def rank_program(g, core, T, topo):
     exp = [((0, 0), rank, 0)]
     for j, s in enumerate(ranks):
         if core in direct[s]:
-            exp.append(((1, direct[s].index(core)), j, _bits(_mask(topo, s, direct[s]))))
+            exp.append(((1, len(direct[s]), direct[s].index(core)), j, _bits(_mask(topo, s, direct[s]))))
         for hi, (h, dests) in enumerate(helpers[s]):
             if core in dests:
-                exp.append(((2, dests.index(core), hi), j, _bits(_mask(topo, h, dests))))
+                exp.append(((2, len(dests), dests.index(core), hi), j, _bits(pass_mask(h, dests))))
     exp.sort()
 
     te, ve = g.tensor, g.vector

@@ -4,10 +4,10 @@ from concourse.mybir import AluOpType
 N = 12
 M = 128
 TK = 64
-NB = 8
+NB = 7
 ND = 5
 CAP = 2
-E_CHIP = 4
+E_CHIP = 8
 E_COPY = 4
 
 SCRATCH = {
@@ -20,8 +20,9 @@ SCRATCH = {
 }
 for _b in range(NB):
     SCRATCH["ps%d" % _b] = ("psum", [128, 512], "float32")
+SCRATCH["pm"] = ("psum", [128, 512], "float32")
 
-SEMAPHORES = (["xl", "wl", "dl", "sent", "st"] + ["a%d" % _j for _j in range(N)]
+SEMAPHORES = (["xl", "wl", "dl", "sent", "st", "vm"] + ["a%d" % _j for _j in range(N)]
               + ["m%d" % _j for _j in range(N)] + ["v%d" % _j for _j in range(N)])
 
 _CACHE = {}
@@ -154,16 +155,20 @@ def rank_program(g, core, T, topo):
     acc = [T.acc0, T.acc1]
     for i in range(N):
         ps = T["ps%d" % (i % NB)][:, 0:TK]
+        a = acc[i % 2]
         ve.wait_ge(T.sem["m%d" % i], 1)
-        if i == 0:
-            ve.tensor_copy(out=acc[0][:], in_=ps).then_inc(T.sem.v0, 1)
+        if i < 2:
+            ve.tensor_copy(out=a[:], in_=ps).then_inc(T.sem["v%d" % i], 1)
         else:
-            ve.wait_ge(T.sem["v%d" % (i - 1)], 1)
-            out = T.yb if i == N - 1 else acc[i % 2]
-            ve.tensor_tensor(out=out[:], in0=acc[(i - 1) % 2][:], in1=ps,
-                             op=AluOpType.max).then_inc(T.sem["v%d" % i], 1)
+            ve.wait_ge(T.sem["v%d" % (i - 2)], 1)
+            out = T.pm[:, 0:TK] if i == N - 1 else a[:]
+            ve.tensor_tensor(out=out, in0=a[:], in1=ps, op=AluOpType.max).then_inc(T.sem["v%d" % i], 1)
+    ve.wait_ge(T.sem["v%d" % (N - 2)], 1)
+    ve.wait_ge(T.sem["v%d" % (N - 1)], 1)
+    ve.tensor_tensor(out=T.yb[:], in0=acc[(N - 2) % 2][:], in1=T.pm[:, 0:TK],
+                     op=AluOpType.max).then_inc(T.sem.vm, 1)
 
-    g.sync.wait_ge(T.sem["v%d" % (N - 1)], 1)
+    g.sync.wait_ge(T.sem.vm, 1)
     g.sync.dma_start(T.y[:], T.yb[:]).then_inc(T.sem.st, 16)
     g.sync.wait_ge(T.sem.st, 16)
     g.wait_ge(T.sem.sent, n)

from concourse.bass import DstId, RemoteDMATransfer
from concourse.mybir import AluOpType

N = 12
M = 128
TK = 64
NB = 7
ND = 5
CAP = 2
E_CHIP = 8
E_COPY = 4

SCRATCH = {
    "wd": ("dram", [128, M], "bfloat16"),
    "wall": ("sbuf", [128, N * M], "bfloat16"),
    "xs": ("sbuf", [128, TK], "bfloat16"),
    "acc0": ("sbuf", [128, TK], "float32"),
    "acc1": ("sbuf", [128, TK], "float32"),
    "yb": ("sbuf", [128, TK], "bfloat16"),
}
for _b in range(NB):
    SCRATCH["ps%d" % _b] = ("psum", [128, 512], "float32")
SCRATCH["pm"] = ("psum", [128, 512], "float32")

SEMAPHORES = (["xl", "wl", "dl", "sent", "st", "vm"] + ["a%d" % _j for _j in range(N)]
              + ["m%d" % _j for _j in range(N)] + ["v%d" % _j for _j in range(N)])

_CACHE = {}


def _route(topo, a, b):
    ca, cb, d = topo.chip(a), topo.chip(b), topo.die(a)
    if ca == cb:
        return []
    if topo.mates(ca, cb):
        return [("mate", ca, d)]
    if topo.same_plane(ca, cb):
        return [("out", ca, d), ("in", cb, d)]
    m = [k for k in range(topo.CHIPS) if topo.mates(ca, k)][0]
    return [("mate", ca, d), ("out", m, d), ("in", cb, d)]


def _plan(ranks, topo):
    load, direct, helpers = {}, {}, {}
    every = range(topo.CHIPS * topo.CORES_PER_CHIP)
    for i, s in enumerate(ranks):
        rot = ranks[i + 1:] + ranks[:i]
        near = [d for d in rot if topo.may_write(s, d)]
        direct[s] = near[:ND]
        far = [d for d in rot if not topo.may_write(s, d)]
        own = [c for c in every if topo.chip(c) == topo.chip(s) and c != s
               and all(topo.may_write(c, d) for d in far)]
        cap = -(-len(far) // len(own))
        opened = {}
        for d in far + near[ND:]:
            best = None
            for h in own:
                if d in far and len(opened.get(h, [])) >= cap:
                    continue
                if d not in far and (len(opened.get(h, [])) >= CAP or topo.die(h) == topo.die(s)):
                    continue
                ls = _route(topo, h, d)
                key = (max([load.get(l, 0) + 1 for l in ls if l[0] == "in"] + [0]),
                       max(load.get(l, 0) + 1 for l in ls), len(opened.get(h, [])), h)
                if best is None or key < best[0]:
                    best = (key, h)
            h = best[1]
            opened.setdefault(h, []).append(d)
            for l in _route(topo, h, d):
                load[l] = load.get(l, 0) + 1
        helpers[s] = sorted(opened.items())
    return direct, helpers


def _bits(mask):
    return bin(mask).count("1")


def _thin(mask, n):
    if n < _bits(mask):
        on = [b for b in range(mask.bit_length()) if (mask >> b) & 1]
        mask = sum(1 << b for b in on[::len(on) // n][:n])
    return mask


def _mask(topo, me, dests):
    mask = topo.mask(me, dests[0])
    for d in dests:
        mask &= topo.mask(me, d)
    return mask


def _send(g, T, topo, dests, j, mask, out):
    ids = [DstId(rid=topo.addr(d)[0], pnc=topo.addr(d)[1]) for d in dests]
    g.remote_dma_fused(
        [RemoteDMATransfer(dst_ids=ids, dma_engine_mask=mask, remote_sem=T.sem["a%d" % j],
                           srcs=[T.wd[:]], dsts=[out for _ in dests], alu_op=0)],
        local_sem=T.sem.sent)
    return _bits(mask)


def rank_program(g, core, T, topo):
    ranks = list(T.cores)
    if "plan" not in _CACHE:
        _CACHE["plan"] = _plan(ranks, topo)
    direct, helpers = _CACHE["plan"]
    rank = T.rank_of(core)

    def chip_mask(s):
        return _thin(_mask(topo, s, [h for h, _ in helpers[s]]) & ~_mask(topo, s, direct[s]), E_CHIP)

    def pass_mask(h, dests):
        return _thin(_mask(topo, h, dests), E_COPY * len(dests))

    if rank is None:
        for j, s in enumerate(ranks):
            for h, dests in helpers[s]:
                if h == core:
                    g.wait_ge(T.sem["a%d" % j], _bits(chip_mask(s)))
                    n = _send(g, T, topo, dests, j, pass_mask(core, dests), T.wall[:, j * M:(j + 1) * M])
                    g.wait_ge(T.sem.sent, n)
        return

    slot = T.wall[:, rank * M:(rank + 1) * M]
    g.scalar.dma_start(T.wd[:], T.w[:]).then_inc(T.sem.dl, 16)
    g.sync.wait_ge(T.sem.dl, 16)
    g.sync.dma_start(T.xs[:], T.x[:]).then_inc(T.sem.xl, 16)
    g.sync.dma_start(slot, T.w[:]).then_inc(T.sem.wl, 16)

    g.wait_ge(T.sem.dl, 16)
    n = _send(g, T, topo, [h for h, _ in helpers[core]], rank, chip_mask(core), T.wd[:])
    n += _send(g, T, topo, direct[core], rank, _mask(topo, core, direct[core]), slot)

    exp = [((0, 0), rank, 0)]
    for j, s in enumerate(ranks):
        if core in direct[s]:
            exp.append(((1, len(direct[s]), direct[s].index(core)), j, _bits(_mask(topo, s, direct[s]))))
        for hi, (h, dests) in enumerate(helpers[s]):
            if core in dests:
                exp.append(((2, len(dests), dests.index(core), hi), j, _bits(pass_mask(h, dests))))
    exp.sort()

    te, ve = g.tensor, g.vector
    te.wait_ge(T.sem.xl, 16)
    for i, (_, j, cnt) in enumerate(exp):
        if j == rank:
            te.wait_ge(T.sem.wl, 16)
        else:
            te.wait_ge(T.sem["a%d" % j], cnt)
        if i >= NB:
            te.wait_ge(T.sem["v%d" % (i - NB)], 1)
        te.matmul(out=T["ps%d" % (i % NB)][:, 0:TK], lhsT=T.wall[:, j * M:(j + 1) * M], rhs=T.xs[:],
                  start=True, stop=True).then_inc(T.sem["m%d" % i], 1)

    acc = [T.acc0, T.acc1]
    for i in range(N):
        ps = T["ps%d" % (i % NB)][:, 0:TK]
        a = acc[i % 2]
        ve.wait_ge(T.sem["m%d" % i], 1)
        if i < 2:
            ve.tensor_copy(out=a[:], in_=ps).then_inc(T.sem["v%d" % i], 1)
        else:
            ve.wait_ge(T.sem["v%d" % (i - 2)], 1)
            out = T.pm[:, 0:TK] if i == N - 1 else a[:]
            ve.tensor_tensor(out=out, in0=a[:], in1=ps, op=AluOpType.max).then_inc(T.sem["v%d" % i], 1)
    ve.wait_ge(T.sem["v%d" % (N - 2)], 1)
    ve.wait_ge(T.sem["v%d" % (N - 1)], 1)
    ve.tensor_tensor(out=T.yb[:], in0=acc[(N - 2) % 2][:], in1=T.pm[:, 0:TK],
                     op=AluOpType.max).then_inc(T.sem.vm, 1)

    g.sync.wait_ge(T.sem.vm, 1)
    g.sync.dma_start(T.y[:], T.yb[:]).then_inc(T.sem.st, 16)
    g.sync.wait_ge(T.sem.st, 16)
    g.wait_ge(T.sem.sent, n)
